import numpy as np
import ml_dtypes


def mxq(x, axis, fmt="e4m3"):
    dtype, down = {"e4m3": (ml_dtypes.float8_e4m3fn, 7), "e5m2": (ml_dtypes.float8_e5m2, 14)}[fmt]
    v = np.moveaxis(np.asarray(x, np.float32).astype(ml_dtypes.bfloat16).astype(np.float64), axis, -1)
    blocks = v.reshape(v.shape[:-1] + (-1, 32))
    amax = np.abs(blocks).max(-1, keepdims=True)
    byte = np.maximum(np.where(amax > 0, np.frexp(amax)[1] - 1 + 127, 0) - down, 1)
    scale = np.exp2(byte - 127.0)
    codes = (blocks / scale).astype(np.float32).astype(dtype).astype(np.float64)
    return np.moveaxis((codes * scale).reshape(v.shape), -1, axis)


WIDE = False


def mx_kscale(k):
    if not WIDE:
        return np.ones(k)
    levels = np.array([10, -10, 5, -5, 0])
    if k % 512:
        return np.exp2(np.random.permutation(np.resize(levels, k // 32))).repeat(32)
    a = np.empty((k // 512, 16))
    for p in range(k // 512):
        a[p, :8] = np.random.permutation(np.resize(levels, 8))
        for g in range(8):
            far = levels[np.abs(levels - a[p, g]) >= 10]
            a[p, g + 8] = far[np.random.randint(len(far))]
    return np.exp2(a.ravel()).repeat(32)


def f64(x):
    return np.asarray(x).astype(np.float64)


def striped(idx):
    return np.tile(idx.reshape(-1, 16).T, (8, 1)).astype(np.uint16)


def unstriped(offs):
    return offs[:16].T.reshape(-1).astype(np.int64)


def striped8(idx):
    return np.concatenate([x.reshape(-1, 16).T for x in idx]).astype(np.uint16)


def runs(offs, k):
    lists = np.stack([offs[16 * r : 16 * r + 16].T.reshape(-1) for r in range(8)]).astype(np.int64)
    return lists[np.arange(k) % 512 // 64]


def pack_weight(w):
    k, n = w.shape
    w = f64(np.asarray(w, np.float32).astype(ml_dtypes.bfloat16)).reshape(k // 32, 32, n)
    amax = np.abs(w).max(1)
    byte = np.clip(np.where(amax > 0, np.frexp(amax)[1] - 1 + 127 - 7, 1), 1, 254)
    scaled = (w * np.exp2(127.0 - byte)[:, None, :]).reshape(k, n).astype(np.float32)
    words = np.ascontiguousarray(scaled.reshape(k // 512, 128, 4, n).transpose(0, 1, 3, 2)).astype(ml_dtypes.float8_e4m3fn).view(np.uint8)
    return words, np.ascontiguousarray(byte.astype(np.uint8).reshape(k // 512, 16, n))


def unpack_weight(words, scales):
    g, p, n, _ = words.shape
    vals = np.ascontiguousarray(words).view(ml_dtypes.float8_e4m3fn).astype(np.float64) * np.repeat(np.exp2(scales.astype(np.float64) - 127.0), 8, axis=1)[..., None]
    return vals.transpose(0, 1, 3, 2).reshape(g * 512, n)


def sigmoid(v):
    return 1.0 / (1.0 + np.exp(-np.maximum(v, -700.0)))

def planes(y):
    n, m = y.shape
    v = y.astype(np.float32).astype(ml_dtypes.bfloat16).astype(np.float64).reshape(n // 32, 32, m)
    top = np.abs(v).max(1)
    byte = np.clip(np.where(top > 0, np.frexp(top)[1] - 1 + 127 - 7, 1), 1, 254)
    codes = (v * np.exp2(127.0 - byte)[:, None, :]).reshape(n, m).astype(np.float32).astype(ml_dtypes.float8_e4m3fn).view(np.uint8)
    words = codes.reshape(n // 512, 128, 4, m).transpose(0, 1, 3, 2)
    return np.ascontiguousarray(words), np.ascontiguousarray(byte.astype(np.uint8).reshape(n // 512, 16, m))


K, T, S, H, U = 512, 2048, 512, 512, 1024


def setup_inputs():
    n = np.random.standard_normal
    s = mx_kscale(K)[:, None]
    u = mx_kscale(S)
    packed_xT = pack_weight(n((K, T)) * s)
    return {
        "x_words": packed_xT[0],
        "x_scales": packed_xT[1],
        "wa": (n((K, H)) / np.sqrt(K) / s).astype(np.float32),
        "wb": (n((K, H)) / np.sqrt(K) / s).astype(np.float32),
        "gt": (np.random.uniform(0.5, 1.5, (S, 1)) * u[:, None]).astype(np.float32),
        "gi": (np.random.uniform(0.5, 1.5, (S, 1)) / u[:, None]).astype(np.float32),
        "mem": n((H, U)).astype(np.float32),
        "offs": striped(np.random.permutation(T)[:S]),
        "two": striped(np.random.permutation(T)[:S]),
        "n1": striped8(np.stack([np.random.permutation(H) for _ in range(8)])),
        "n2": striped8(np.stack([np.random.permutation(H) for _ in range(8)])),
        "n3": striped8(np.stack([np.random.permutation(U)[:H] for _ in range(8)])),
    }


def reference(x_words, x_scales, wa, wb, gt, gi, mem, offs, two, n1, n2, n3):
    xq = unpack_weight(x_words, x_scales)[:, unstriped(offs)]
    a = xq.T @ mxq(f64(wa), 0, "e4m3")
    x_two = unpack_weight(x_words, x_scales)[:, unstriped(two)]
    b = x_two.T @ mxq(f64(wb), 0, "e4m3")
    z = f64(gt) * ((a + a[np.arange(S)[:, None], runs(n1, S)]) * (sigmoid(b + b[np.arange(S)[:, None], runs(n2, S)])))
    z2 = f64(gi) * b
    cv = 0.0625 * ((mxq(z, 0, "e4m3").T @ mxq(z2, 0, "e4m3")))
    nw = np.maximum(cv, 0.5 * (f64(mem)[np.arange(H)[:, None], runs(n3, H)]))
    out = f64(mem).copy()
    out[np.arange(H)[:, None], runs(n3, H)] = nw
    return (out,) + planes(out)

@@ -1,0 +1,250 @@
+from contextlib import ExitStack
+
+import concourse.mybir as mybir
+
+K, T, S, H, U = 512, 2048, 512, 512, 1024
+FLOPS = 3 * 2 * 512 * 512 * 512
+
+F32 = mybir.dt.float32
+BF16 = mybir.dt.bfloat16
+I32 = mybir.dt.int32
+U32 = mybir.dt.uint32
+U16 = mybir.dt.uint16
+U8 = mybir.dt.uint8
+FP8X4 = mybir.dt.float8_e4m3fn_x4
+ALU = mybir.AluOpType
+ACT = mybir.ActivationFunctionType
+
+P = 128
+PACK = 4
+HALF = 256
+LCOL = 16
+
+
+def tile_picked_momttriebpagex_none_po_kernel(
+    tc, x_words, x_scales, wa, wb, gt, gi, mem, offs, two, n1, n2, n3, out_0, out_1, out_2
+):
+    nc = tc.nc
+    with ExitStack() as ctx:
+        keep = ctx.enter_context(tc.tile_pool(name="keep", bufs=1))
+        psum = ctx.enter_context(tc.psum_pool(name="psum", bufs=1))
+
+        def sb(name, shape, dtype, tag=""):
+            return keep.tile(shape, dtype, name=name, tag=tag or name, align_bytes=64)
+
+        def load_list(name, src):
+            tile = keep.tile([P, S // LCOL], U16, name=name)
+            nc.sync.dma_start(tile[:], src)
+            return tile
+
+        xw = sb("xw", [P, T], U32)
+        xs = sb("xs", [P, T], U8)
+        nc.vector.memset(xs[:].bitcast(I32), 0)
+        two_t = load_list("two_t", two)
+
+        def load_weight(name, w, h):
+            raw = sb(f"{name}_raw{h}", [P, PACK, HALF], F32)
+            nc.sync.dma_start(raw[:], w.rearrange("(p j) n -> p j n", j=PACK)[:, :, h * HALF : (h + 1) * HALF])
+            return raw
+
+        wb_raw = [load_weight("wb", wb, 0)]
+        for q in range(4):
+            nc.sync.dma_start(xs[32 * q : 32 * q + 4, :].bitcast(I32), x_scales[0, 4 * q : 4 * q + 4, :].bitcast(I32))
+        offs_t = load_list("offs_t", offs)
+        n2_t = load_list("n2_t", n2)
+        wb_raw.append(load_weight("wb", wb, 1))
+        nc.sync.dma_start(xw[:].bitcast(I32), x_words[0].rearrange("p n t -> p (n t)").bitcast(I32))
+        wa_raw = [load_weight("wa", wa, h) for h in range(2)]
+        n1_t = load_list("n1_t", n1)
+        gt_t = sb("gt_t", [P, PACK], F32)
+        gi_t = sb("gi_t", [P, PACK], F32)
+        nc.sync.dma_start(gi_t[:], gi.rearrange("(p t) o -> p (t o)", t=PACK))
+        nc.sync.dma_start(gt_t[:], gt.rearrange("(p t) o -> p (t o)", t=PACK))
+        n3_t = load_list("n3_t", n3)
+        page = []
+        for t in range(PACK):
+            w = sb(f"page{t}", [P, U], F32)
+            nc.sync.dma_start(w[:], mem.rearrange("(p t) u -> p t u", t=PACK)[:, t, :])
+            page.append(w)
+
+        def pick(name, table, lst, dtype):
+            picked = sb(name, [P, S], dtype)
+            nc.vector.tensor_copy(picked[:].rearrange("p (t m) -> p m t", t=PACK), table[:].indirect(lst[:]))
+            return picked
+
+        def regroup(engine, name, raw):
+            grouped = sb(name, [P, HALF, PACK], BF16)
+            dst = grouped[:].rearrange("p (c i) j -> p c j i", i=4)
+            src = raw[:].rearrange("p j (c i) -> p c j i", i=4)
+            if engine == "s":
+                nc.scalar.copy(dst, src)
+            else:
+                nc.vector.tensor_copy(dst, src)
+            return grouped
+
+        def quantise(codes, scales, cols, grouped):
+            nc.vector.quantize_mx(
+                out=codes[:, cols].bitcast(FP8X4), scales=scales[:, cols], in_=grouped.rearrange("p c j -> p (c j)")
+            )
+
+        halves = [slice(h * HALF, (h + 1) * HALF) for h in range(2)]
+        lhalves = [slice(h * HALF // LCOL, (h + 1) * HALF // LCOL) for h in range(2)]
+
+        def product(tag, lhs_c, lhs_s, rhs_c, rhs_s, t):
+            bank = psum.tile([P, H], F32, name=f"{tag}{t}", tag=f"bank_{tag[0]}{t}")
+            cols = slice(t * P, (t + 1) * P)
+            nc.tensor.matmul_mx(
+                out=bank[:], lhsT=lhs_c[:, cols].bitcast(FP8X4), lhsT_scale=lhs_s[:, cols],
+                rhs=rhs_c[:].bitcast(FP8X4), rhs_scale=rhs_s[:], start=True, stop=True,
+            )
+            return bank
+
+        wb_c, wb_s = sb("wb_c", [P, H], U32), sb("wb_s", [P, H], U8)
+        wa_c, wa_s = sb("wa_c", [P, H], U32), sb("wa_s", [P, H], U8)
+        xb_s = pick("xb_s", xs, two_t, U8)
+        xa_s = pick("xa_s", xs, offs_t, U8)
+        wb_g = [regroup("s", f"wb_g{h}", wb_raw[h]) for h in range(2)]
+        quantise(wb_c, wb_s, halves[0], wb_g[0][:])
+        quantise(wb_c, wb_s, halves[1], wb_g[1][:])
+        xb_w = pick("xb_w", xw, two_t, U32)
+        b_ps = [product("b", xb_w, xb_s, wb_c, wb_s, t) for t in range(PACK)]
+        xa_w = pick("xa_w", xw, offs_t, U32)
+        wa_g = [regroup("sv"[h], f"wa_g{h}", wa_raw[h]) for h in range(2)]
+        for h in range(2):
+            quantise(wa_c, wa_s, halves[h], wa_g[h][:])
+        a_ps = [product("a", xa_w, xa_s, wa_c, wa_s, t) for t in range(PACK)]
+
+        def gather(engine, out, window, lst):
+            if engine == "s":
+                nc.scalar.activation(out, window.indirect(lst), ACT.Copy)
+            else:
+                nc.vector.tensor_copy(out, window.indirect(lst))
+
+        gate = [sb(f"gate{h}", [P, PACK, HALF], F32) for h in range(2)]
+        asum = [sb(f"asum{h}", [P, PACK, HALF], F32) for h in range(2)]
+        z2_rows = sb("z2_rows", [P, PACK, H], BF16)
+        b_sb = [sb(f"b{t}", [P, H], F32) for t in range(PACK)]
+        a_sb = [sb(f"a{t}", [P, H], F32) for t in range(PACK)]
+        bgot = [sb(f"bgot{t}", [P, H], F32) for t in range(PACK)]
+        agot = [sb(f"agot{t}", [P, H], F32) for t in range(PACK)]
+        bsum = [sb(f"bsum{t}", [P, H], F32) for t in range(PACK)]
+        old = []
+        z2_g = sb("z2_g", [P, H, PACK], BF16)
+        z2_c = sb("z2_c", [P, H], U32)
+        z2_s = sb("z2_s", [P, H], U8)
+        z_g = sb("z_g", [P, PACK, P, PACK], BF16)
+
+        def b_fetch(t):
+            nc.scalar.copy(b_sb[t][:], b_ps[t][:])
+            for h in range(2):
+                gather("s", bgot[t][:, halves[h]], b_sb[t][:], n2_t[:, lhalves[h]])
+
+        def b_add(t):
+            nc.vector.tensor_tensor(bsum[t][:], bgot[t][:], b_sb[t][:], ALU.add)
+
+        def z2_row(t):
+            nc.vector.tensor_scalar(z2_rows[:, t, :], b_sb[t][:], gi_t[:, t : t + 1], None, ALU.mult)
+
+        def a_copy(engine, t):
+            if engine == "s":
+                nc.scalar.activation(a_sb[t][:], a_ps[t][:], ACT.Copy, scale=gt_t[:, t : t + 1])
+            else:
+                nc.vector.tensor_scalar(a_sb[t][:], a_ps[t][:], gt_t[:, t : t + 1], None, ALU.mult)
+
+        def a_gather(engine, t, h):
+            gather(engine, agot[t][:, halves[h]], a_sb[t][:], n1_t[:, lhalves[h]])
+
+        def a_add(t, h):
+            nc.vector.tensor_tensor(asum[h][:, t, :], agot[t][:, halves[h]], a_sb[t][:, halves[h]], ALU.add)
+
+        def old_fetch(u):
+            old.append(sb(f"old{u}", [P, H], F32, tag=f"bsum{u}"))
+            nc.scalar.activation(old[u][:], page[u][:].indirect(n3_t[:]), ACT.Copy, scale=0.5)
+
+        b_fetch(0)
+        z2_row(0)
+        b_add(0)
+        a_copy("v", 0)
+        b_fetch(1)
+        for h in range(2):
+            a_gather("v", 0, h)
+        a_copy("s", 1)
+        b_add(1)
+        z2_row(1)
+        b_fetch(2)
+        for h in range(2):
+            a_add(0, h)
+        for h in range(2):
+            a_gather("v", 1, h)
+        b_add(2)
+        z2_row(2)
+        b_fetch(3)
+        for h in range(2):
+            a_add(1, h)
+        b_add(3)
+        z2_row(3)
+        a_copy("s", 2)
+        a_copy("s", 3)
+        nc.vector.tensor_copy(
+            z2_g[:].rearrange("p (c i) t -> p c t i", i=4), z2_rows[:].rearrange("p t (c i) -> p c t i", i=4)
+        )
+        quantise(z2_c, z2_s, slice(0, H), z2_g[:])
+        for h in range(2):
+            for t in (2, 3):
+                a_gather("s", t, h)
+                a_add(t, h)
+            for t in range(PACK):
+                nc.scalar.activation(gate[h][:, t, :], bsum[t][:, halves[h]], ACT.Sigmoid)
+            nc.vector.tensor_tensor(
+                z_g[:, :, h * 64 : (h + 1) * 64, :].rearrange("p u m t -> p m t u"),
+                asum[h][:].rearrange("p t (m u) -> p m t u", u=PACK),
+                gate[h][:].rearrange("p t (m u) -> p m t u", u=PACK),
+                ALU.mult,
+            )
+        old_fetch(0)
+        z_c = sb("z_c", [P, H], U32)
+        z_s = sb("z_s", [P, H], U8)
+        for u in range(PACK):
+            cols = slice(u * P, (u + 1) * P)
+            nc.vector.quantize_mx(
+                out=z_c[:, cols].bitcast(FP8X4), scales=z_s[:, cols], in_=z_g[:, u, :, :].rearrange("p m t -> p (m t)")
+            )
+        cv_ps = [product("bcv", z_c, z_s, z2_c, z2_s, u) for u in range(PACK)]
+
+        for u in range(1, PACK):
+            old_fetch(u)
+        parts = [slice(0, 640), slice(640, U)]
+        widths = [c.stop - c.start for c in parts]
+        y_rows = [[sb(f"y_rows{i}{e}", [P, 2, widths[i]], BF16) for e in range(2)] for i in range(2)]
+        y_g = [sb(f"y_g{i}", [P, widths[i], PACK], BF16) for i in range(2)]
+        y_c = sb("y_c", [P, U], U32)
+        y_s = sb("y_s", [P, U], U8)
+        words_out = out_1[0].rearrange("p n t -> p (n t)").bitcast(I32)
+
+        def cast(copy, i, u):
+            copy(y_rows[i][u // 2][:, u % 2, :], page[u][:, parts[i]])
+
+        def weave(copy, i, e):
+            copy(y_g[i][:, :, 2 * e : 2 * e + 2], y_rows[i][e][:].rearrange("p r c -> p c r"))
+
+        for u in range(PACK):
+            new = sb(f"new{u}", [P, H], F32)
+            nc.vector.scalar_tensor_tensor(new[:], cv_ps[u][:], 0.0625, old[u][:], ALU.mult, ALU.max)
+            nc.vector.tensor_copy(page[u][:].indirect(n3_t[:]), new[:])
+            nc.sync.dma_start(out_0.rearrange("(p t) u -> p t u", t=PACK)[:, u, :], page[u][:])
+            if u < PACK - 1:
+                for i in range(2):
+                    cast(nc.scalar.copy, i, u)
+            if u == 1:
+                for i in range(2):
+                    weave(nc.scalar.copy, i, 0)
+        cast(nc.scalar.copy, 1, PACK - 1)
+        weave(nc.scalar.copy, 1, 1)
+        cast(nc.vector.tensor_copy, 0, PACK - 1)
+        weave(nc.vector.tensor_copy, 0, 1)
+        for i, lo, hi in ((0, 0, 512), (0, 512, 640), (1, 640, U)):
+            cols = slice(lo, hi)
+            quantise(y_c, y_s, cols, y_g[i][:, lo - parts[i].start : hi - parts[i].start, :])
+            nc.sync.dma_start(words_out[:, cols], y_c[:, cols].bitcast(I32))
+        for q in range(4):
+            nc.scalar.dma_start(out_2[0, 4 * q : 4 * q + 4, :].bitcast(I32), y_s[32 * q : 32 * q + 4, :].bitcast(I32))

@@ -41,20 +41,22 @@ def tile_picked_momttriebpagex_none_po_kernel(
         xs = sb("xs", [P, T], U8)
         nc.vector.memset(xs[:].bitcast(I32), 0)
         two_t = load_list("two_t", two)
+        offs_t = load_list("offs_t", offs)
 
-        def load_weight(name, w, h):
-            raw = sb(f"{name}_raw{h}", [P, PACK, HALF], F32)
-            nc.sync.dma_start(raw[:], w.rearrange("(p j) n -> p j n", j=PACK)[:, :, h * HALF : (h + 1) * HALF])
+        def load_weight(name, w, cols):
+            raw = sb(name, [P, PACK, cols.stop - cols.start], F32)
+            nc.sync.dma_start(raw[:], w.rearrange("(p j) n -> p j n", j=PACK)[:, :, cols])
             return raw
 
-        wb_raw = [load_weight("wb", wb, 0)]
+        wb_cols = [slice(0, 384), slice(384, H)]
+        wa_cols = [slice(0, HALF), slice(HALF, H)]
+        wb_raw = [load_weight("wb_raw0", wb, wb_cols[0])]
         for q in range(4):
             nc.sync.dma_start(xs[32 * q : 32 * q + 4, :].bitcast(I32), x_scales[0, 4 * q : 4 * q + 4, :].bitcast(I32))
-        offs_t = load_list("offs_t", offs)
         n2_t = load_list("n2_t", n2)
-        wb_raw.append(load_weight("wb", wb, 1))
+        wb_raw.append(load_weight("wb_raw1", wb, wb_cols[1]))
         nc.sync.dma_start(xw[:].bitcast(I32), x_words[0].rearrange("p n t -> p (n t)").bitcast(I32))
-        wa_raw = [load_weight("wa", wa, h) for h in range(2)]
+        wa_raw = [load_weight(f"wa_raw{h}", wa, wa_cols[h]) for h in range(2)]
         n1_t = load_list("n1_t", n1)
         gt_t = sb("gt_t", [P, PACK], F32)
         gi_t = sb("gi_t", [P, PACK], F32)
@@ -67,13 +69,15 @@ def tile_picked_momttriebpagex_none_po_kernel(
             nc.sync.dma_start(w[:], mem.rearrange("(p t) u -> p t u", t=PACK)[:, t, :])
             page.append(w)
 
+        warm = sb("warm", [P, 1], F32)
+        nc.scalar.activation(warm[:], wb_raw[0][:, 0, 0:1], ACT.Sigmoid)
         def pick(name, table, lst, dtype):
             picked = sb(name, [P, S], dtype)
             nc.vector.tensor_copy(picked[:].rearrange("p (t m) -> p m t", t=PACK), table[:].indirect(lst[:]))
             return picked
 
         def regroup(engine, name, raw):
-            grouped = sb(name, [P, HALF, PACK], BF16)
+            grouped = sb(name, [P, raw.shape[2], PACK], BF16)
             dst = grouped[:].rearrange("p (c i) j -> p c j i", i=4)
             src = raw[:].rearrange("p j (c i) -> p c j i", i=4)
             if engine == "s":
@@ -104,8 +108,8 @@ def tile_picked_momttriebpagex_none_po_kernel(
         xb_s = pick("xb_s", xs, two_t, U8)
         xa_s = pick("xa_s", xs, offs_t, U8)
         wb_g = [regroup("s", f"wb_g{h}", wb_raw[h]) for h in range(2)]
-        quantise(wb_c, wb_s, halves[0], wb_g[0][:])
-        quantise(wb_c, wb_s, halves[1], wb_g[1][:])
+        quantise(wb_c, wb_s, wb_cols[0], wb_g[0][:])
+        quantise(wb_c, wb_s, wb_cols[1], wb_g[1][:])
         xb_w = pick("xb_w", xw, two_t, U32)
         b_ps = [product("b", xb_w, xb_s, wb_c, wb_s, t) for t in range(PACK)]
         xa_w = pick("xa_w", xw, offs_t, U32)
@@ -121,26 +125,28 @@ def tile_picked_momttriebpagex_none_po_kernel(
                 nc.vector.tensor_copy(out, window.indirect(lst))
 
         gate = [sb(f"gate{h}", [P, PACK, HALF], F32) for h in range(2)]
-        asum = [sb(f"asum{h}", [P, PACK, HALF], F32) for h in range(2)]
-        z2_rows = sb("z2_rows", [P, PACK, H], BF16)
-        b_sb = [sb(f"b{t}", [P, H], F32) for t in range(PACK)]
+        asum = sb("asum", [P, 2, PACK, HALF], F32)
+        z2_rows = sb("z2_rows", [P, PACK, H], BF16, tag="wa_raw1")
+        b_sb = [sb(f"b{t}", [P, H], F32, tag=["wa_raw0", "wa_g0", "", ""][t]) for t in range(PACK)]
         a_sb = [sb(f"a{t}", [P, H], F32) for t in range(PACK)]
         bgot = [sb(f"bgot{t}", [P, H], F32) for t in range(PACK)]
         agot = [sb(f"agot{t}", [P, H], F32) for t in range(PACK)]
-        bsum = [sb(f"bsum{t}", [P, H], F32) for t in range(PACK)]
+        bsum = sb("bsum", [P, PACK, H], F32, tag="wa_g1")
         old = []
         z2_g = sb("z2_g", [P, H, PACK], BF16)
         z2_c = sb("z2_c", [P, H], U32)
         z2_s = sb("z2_s", [P, H], U8)
         z_g = sb("z_g", [P, PACK, P, PACK], BF16)
 
-        def b_fetch(t):
+        def b_copy(t):
             nc.scalar.copy(b_sb[t][:], b_ps[t][:])
+
+        def b_gather(t):
             for h in range(2):
                 gather("s", bgot[t][:, halves[h]], b_sb[t][:], n2_t[:, lhalves[h]])
 
         def b_add(t):
-            nc.vector.tensor_tensor(bsum[t][:], bgot[t][:], b_sb[t][:], ALU.add)
+            nc.vector.tensor_tensor(bsum[:, t, :], bgot[t][:], b_sb[t][:], ALU.add)
 
         def z2_row(t):
             nc.vector.tensor_scalar(z2_rows[:, t, :], b_sb[t][:], gi_t[:, t : t + 1], None, ALU.mult)
@@ -155,49 +161,57 @@ def tile_picked_momttriebpagex_none_po_kernel(
             gather(engine, agot[t][:, halves[h]], a_sb[t][:], n1_t[:, lhalves[h]])
 
         def a_add(t, h):
-            nc.vector.tensor_tensor(asum[h][:, t, :], agot[t][:, halves[h]], a_sb[t][:, halves[h]], ALU.add)
+            nc.vector.tensor_tensor(asum[:, h, t, :], agot[t][:, halves[h]], a_sb[t][:, halves[h]], ALU.add)
+
+        def a_add_both(t):
+            split = "p (h c) -> p h c"
+            nc.vector.tensor_tensor(
+                asum[:, :, t, :], agot[t][:].rearrange(split, h=2), a_sb[t][:].rearrange(split, h=2), ALU.add
+            )
 
         def old_fetch(u):
-            old.append(sb(f"old{u}", [P, H], F32, tag=f"bsum{u}"))
+            old.append(sb(f"old{u}", [P, H], F32, tag=["wa_g1", "gate0", "gate1", "asum"][u]))
             nc.scalar.activation(old[u][:], page[u][:].indirect(n3_t[:]), ACT.Copy, scale=0.5)
 
-        b_fetch(0)
+        b_copy(0)
+        b_copy(1)
         z2_row(0)
-        b_add(0)
+        z2_row(1)
+        b_gather(0)
         a_copy("v", 0)
-        b_fetch(1)
+        b_add(0)
+        b_copy(2)
         for h in range(2):
             a_gather("v", 0, h)
-        a_copy("s", 1)
+        b_gather(1)
         b_add(1)
-        z2_row(1)
-        b_fetch(2)
-        for h in range(2):
-            a_add(0, h)
+        b_copy(3)
+        a_copy("s", 1)
+        z2_row(2)
+        a_add_both(0)
+        b_gather(2)
         for h in range(2):
             a_gather("v", 1, h)
         b_add(2)
-        z2_row(2)
-        b_fetch(3)
-        for h in range(2):
-            a_add(1, h)
-        b_add(3)
         z2_row(3)
+        b_gather(3)
+        a_add_both(1)
+        b_add(3)
         a_copy("s", 2)
         a_copy("s", 3)
         nc.vector.tensor_copy(
             z2_g[:].rearrange("p (c i) t -> p c t i", i=4), z2_rows[:].rearrange("p t (c i) -> p c t i", i=4)
         )
-        quantise(z2_c, z2_s, slice(0, H), z2_g[:])
         for h in range(2):
             for t in (2, 3):
                 a_gather("s", t, h)
                 a_add(t, h)
-            for t in range(PACK):
-                nc.scalar.activation(gate[h][:, t, :], bsum[t][:, halves[h]], ACT.Sigmoid)
+                if h == 0 and t == 2:
+                    quantise(z2_c, z2_s, slice(0, H), z2_g[:])
+            nc.scalar.activation(gate[h][:], bsum[:, :, halves[h]], ACT.Sigmoid)
             nc.vector.tensor_tensor(
                 z_g[:, :, h * 64 : (h + 1) * 64, :].rearrange("p u m t -> p m t u"),
-                asum[h][:].rearrange("p t (m u) -> p m t u", u=PACK),
+                asum[:, h, :, :].rearrange("p t (m u) -> p m t u", u=PACK),
                 gate[h][:].rearrange("p t (m u) -> p m t u", u=PACK),
                 ALU.mult,
             )

@@ -126,12 +126,12 @@ def tile_picked_momttriebpagex_none_po_kernel(
 
         gate = [sb(f"gate{h}", [P, PACK, HALF], F32) for h in range(2)]
         asum = sb("asum", [P, 2, PACK, HALF], F32)
-        z2_rows = sb("z2_rows", [P, PACK, H], BF16, tag="wa_raw1")
+        z2_rows = sb("z2_rows", [P, PACK, H], BF16, tag="wa_g1")
         b_sb = [sb(f"b{t}", [P, H], F32, tag=["wa_raw0", "wa_g0", "", ""][t]) for t in range(PACK)]
         a_sb = [sb(f"a{t}", [P, H], F32) for t in range(PACK)]
         bgot = [sb(f"bgot{t}", [P, H], F32) for t in range(PACK)]
         agot = [sb(f"agot{t}", [P, H], F32) for t in range(PACK)]
-        bsum = sb("bsum", [P, PACK, H], F32, tag="wa_g1")
+        bsum = sb("bsum", [P, PACK, H], F32, tag="wa_raw1")
         old = []
         z2_g = sb("z2_g", [P, H, PACK], BF16)
         z2_c = sb("z2_c", [P, H], U32)
@@ -146,10 +146,10 @@ def tile_picked_momttriebpagex_none_po_kernel(
                 gather("s", bgot[t][:, halves[h]], b_sb[t][:], n2_t[:, lhalves[h]])
 
         def b_add(t):
-            nc.vector.tensor_tensor(bsum[:, t, :], bgot[t][:], b_sb[t][:], ALU.add)
+            nc.vector.tensor_tensor(bsum[:, t, :], b_ps[t][:], bgot[t][:], ALU.add)
 
         def z2_row(t):
-            nc.vector.tensor_scalar(z2_rows[:, t, :], b_sb[t][:], gi_t[:, t : t + 1], None, ALU.mult)
+            nc.gpsimd.tensor_scalar(z2_rows[:, t, :], b_sb[t][:], gi_t[:, t : t + 1], 0.0, ALU.mult, ALU.add)
 
         def a_copy(engine, t):
             if engine == "s":
@@ -161,17 +161,32 @@ def tile_picked_momttriebpagex_none_po_kernel(
             gather(engine, agot[t][:, halves[h]], a_sb[t][:], n1_t[:, lhalves[h]])
 
         def a_add(t, h):
-            nc.vector.tensor_tensor(asum[:, h, t, :], agot[t][:, halves[h]], a_sb[t][:, halves[h]], ALU.add)
+            nc.vector.scalar_tensor_tensor(
+                asum[:, h, t, :], a_ps[t][:, halves[h]], gt_t[:, t : t + 1], agot[t][:, halves[h]], ALU.mult, ALU.add
+            )
 
         def a_add_both(t):
             split = "p (h c) -> p h c"
-            nc.vector.tensor_tensor(
-                asum[:, :, t, :], agot[t][:].rearrange(split, h=2), a_sb[t][:].rearrange(split, h=2), ALU.add
+            nc.vector.scalar_tensor_tensor(
+                asum[:, :, t, :], a_ps[t][:].rearrange(split, h=2), gt_t[:, t : t + 1],
+                agot[t][:].rearrange(split, h=2), ALU.mult, ALU.add,
             )
 
         def old_fetch(u):
-            old.append(sb(f"old{u}", [P, H], F32, tag=["wa_g1", "gate0", "gate1", "asum"][u]))
+            old.append(sb(f"old{u}", [P, H], F32, tag=["wa_raw1", "gate0", "gate1", "asum"][u]))
             nc.scalar.activation(old[u][:], page[u][:].indirect(n3_t[:]), ACT.Copy, scale=0.5)
+
+        def a_gather_both(t):
+            for h in range(2):
+                a_gather("v", t, h)
+
+        def z_half(h):
+            nc.vector.tensor_tensor(
+                z_g[:, :, h * 64 : (h + 1) * 64, :].rearrange("p u m t -> p m t u"),
+                asum[:, h, :, :].rearrange("p t (m u) -> p m t u", u=PACK),
+                gate[h][:].rearrange("p t (m u) -> p m t u", u=PACK),
+                ALU.mult,
+            )
 
         b_copy(0)
         b_copy(1)
@@ -179,42 +194,34 @@ def tile_picked_momttriebpagex_none_po_kernel(
         z2_row(1)
         b_gather(0)
         a_copy("v", 0)
+        a_gather_both(0)
         b_add(0)
         b_copy(2)
-        for h in range(2):
-            a_gather("v", 0, h)
+        z2_row(2)
         b_gather(1)
+        a_copy("v", 2)
+        a_add_both(0)
         b_add(1)
         b_copy(3)
-        a_copy("s", 1)
-        z2_row(2)
-        a_add_both(0)
-        b_gather(2)
-        for h in range(2):
-            a_gather("v", 1, h)
-        b_add(2)
         z2_row(3)
+        nc.gpsimd.tensor_scalar(z2_g[:], z2_rows[:].rearrange("p t c -> p c t"), 1.0, 0.0, ALU.mult, ALU.add)
+        a_copy("s", 1)
+        b_gather(2)
+        a_gather_both(1)
+        b_add(2)
         b_gather(3)
-        a_add_both(1)
+        a_gather_both(2)
         b_add(3)
-        a_copy("s", 2)
         a_copy("s", 3)
-        nc.vector.tensor_copy(
-            z2_g[:].rearrange("p (c i) t -> p c t i", i=4), z2_rows[:].rearrange("p t (c i) -> p c t i", i=4)
-        )
+        a_add_both(1)
+        a_add_both(2)
         for h in range(2):
-            for t in (2, 3):
-                a_gather("s", t, h)
-                a_add(t, h)
-                if h == 0 and t == 2:
-                    quantise(z2_c, z2_s, slice(0, H), z2_g[:])
+            a_gather("s", 3, h)
+            a_add(3, h)
             nc.scalar.activation(gate[h][:], bsum[:, :, halves[h]], ACT.Sigmoid)
-            nc.vector.tensor_tensor(
-                z_g[:, :, h * 64 : (h + 1) * 64, :].rearrange("p u m t -> p m t u"),
-                asum[:, h, :, :].rearrange("p t (m u) -> p m t u", u=PACK),
-                gate[h][:].rearrange("p t (m u) -> p m t u", u=PACK),
-                ALU.mult,
-            )
+            z_half(h)
+            if h == 0:
+                quantise(z2_c, z2_s, slice(0, H), z2_g[:])
         old_fetch(0)
         z_c = sb("z_c", [P, H], U32)
         z_s = sb("z_s", [P, H], U8)

from contextlib import ExitStack

import concourse.mybir as mybir

K, T, S, H, U = 512, 2048, 512, 512, 1024
FLOPS = 3 * 2 * 512 * 512 * 512

F32 = mybir.dt.float32
BF16 = mybir.dt.bfloat16
I32 = mybir.dt.int32
U32 = mybir.dt.uint32
U16 = mybir.dt.uint16
U8 = mybir.dt.uint8
FP8X4 = mybir.dt.float8_e4m3fn_x4
ALU = mybir.AluOpType
ACT = mybir.ActivationFunctionType

P = 128
PACK = 4
HALF = 256
LCOL = 16


def tile_picked_momttriebpagex_none_po_kernel(
    tc, x_words, x_scales, wa, wb, gt, gi, mem, offs, two, n1, n2, n3, out_0, out_1, out_2
):
    nc = tc.nc
    with ExitStack() as ctx:
        keep = ctx.enter_context(tc.tile_pool(name="keep", bufs=1))
        psum = ctx.enter_context(tc.psum_pool(name="psum", bufs=1))

        def sb(name, shape, dtype, tag=""):
            return keep.tile(shape, dtype, name=name, tag=tag or name, align_bytes=64)

        def load_list(name, src):
            tile = keep.tile([P, S // LCOL], U16, name=name)
            nc.sync.dma_start(tile[:], src)
            return tile

        xw = sb("xw", [P, T], U32)
        xs = sb("xs", [P, T], U8)
        nc.vector.memset(xs[:].bitcast(I32), 0)
        two_t = load_list("two_t", two)
        offs_t = load_list("offs_t", offs)

        def load_weight(name, w, cols):
            raw = sb(name, [P, PACK, cols.stop - cols.start], F32)
            nc.sync.dma_start(raw[:], w.rearrange("(p j) n -> p j n", j=PACK)[:, :, cols])
            return raw

        wb_cols = [slice(0, 384), slice(384, H)]
        wa_cols = [slice(0, HALF), slice(HALF, H)]
        wb_raw = [load_weight("wb_raw0", wb, wb_cols[0])]
        for q in range(4):
            nc.sync.dma_start(xs[32 * q : 32 * q + 4, :].bitcast(I32), x_scales[0, 4 * q : 4 * q + 4, :].bitcast(I32))
        n2_t = load_list("n2_t", n2)
        wb_raw.append(load_weight("wb_raw1", wb, wb_cols[1]))
        nc.sync.dma_start(xw[:].bitcast(I32), x_words[0].rearrange("p n t -> p (n t)").bitcast(I32))
        wa_raw = [load_weight(f"wa_raw{h}", wa, wa_cols[h]) for h in range(2)]
        n1_t = load_list("n1_t", n1)
        gt_t = sb("gt_t", [P, PACK], F32)
        gi_t = sb("gi_t", [P, PACK], F32)
        nc.sync.dma_start(gi_t[:], gi.rearrange("(p t) o -> p (t o)", t=PACK))
        nc.sync.dma_start(gt_t[:], gt.rearrange("(p t) o -> p (t o)", t=PACK))
        n3_t = load_list("n3_t", n3)
        page = []
        for t in range(PACK):
            w = sb(f"page{t}", [P, U], F32)
            nc.sync.dma_start(w[:], mem.rearrange("(p t) u -> p t u", t=PACK)[:, t, :])
            page.append(w)

        warm = sb("warm", [P, 1], F32)
        nc.scalar.activation(warm[:], wb_raw[0][:, 0, 0:1], ACT.Sigmoid)
        def pick(name, table, lst, dtype):
            picked = sb(name, [P, S], dtype)
            nc.vector.tensor_copy(picked[:].rearrange("p (t m) -> p m t", t=PACK), table[:].indirect(lst[:]))
            return picked

        def regroup(engine, name, raw):
            grouped = sb(name, [P, raw.shape[2], PACK], BF16)
            dst = grouped[:].rearrange("p (c i) j -> p c j i", i=4)
            src = raw[:].rearrange("p j (c i) -> p c j i", i=4)
            if engine == "s":
                nc.scalar.copy(dst, src)
            else:
                nc.vector.tensor_copy(dst, src)
            return grouped

        def quantise(codes, scales, cols, grouped):
            nc.vector.quantize_mx(
                out=codes[:, cols].bitcast(FP8X4), scales=scales[:, cols], in_=grouped.rearrange("p c j -> p (c j)")
            )

        halves = [slice(h * HALF, (h + 1) * HALF) for h in range(2)]
        lhalves = [slice(h * HALF // LCOL, (h + 1) * HALF // LCOL) for h in range(2)]

        def product(tag, lhs_c, lhs_s, rhs_c, rhs_s, t):
            bank = psum.tile([P, H], F32, name=f"{tag}{t}", tag=f"bank_{tag[0]}{t}")
            cols = slice(t * P, (t + 1) * P)
            nc.tensor.matmul_mx(
                out=bank[:], lhsT=lhs_c[:, cols].bitcast(FP8X4), lhsT_scale=lhs_s[:, cols],
                rhs=rhs_c[:].bitcast(FP8X4), rhs_scale=rhs_s[:], start=True, stop=True,
            )
            return bank

        wb_c, wb_s = sb("wb_c", [P, H], U32), sb("wb_s", [P, H], U8)
        wa_c, wa_s = sb("wa_c", [P, H], U32), sb("wa_s", [P, H], U8)
        xb_s = pick("xb_s", xs, two_t, U8)
        xa_s = pick("xa_s", xs, offs_t, U8)
        wb_g = [regroup("s", f"wb_g{h}", wb_raw[h]) for h in range(2)]
        quantise(wb_c, wb_s, wb_cols[0], wb_g[0][:])
        quantise(wb_c, wb_s, wb_cols[1], wb_g[1][:])
        xb_w = pick("xb_w", xw, two_t, U32)
        b_ps = [product("b", xb_w, xb_s, wb_c, wb_s, t) for t in range(PACK)]
        xa_w = pick("xa_w", xw, offs_t, U32)
        wa_g = [regroup("sv"[h], f"wa_g{h}", wa_raw[h]) for h in range(2)]
        for h in range(2):
            quantise(wa_c, wa_s, halves[h], wa_g[h][:])
        a_ps = [product("a", xa_w, xa_s, wa_c, wa_s, t) for t in range(PACK)]

        def gather(engine, out, window, lst):
            if engine == "s":
                nc.scalar.activation(out, window.indirect(lst), ACT.Copy)
            else:
                nc.vector.tensor_copy(out, window.indirect(lst))

        gate = [sb(f"gate{h}", [P, PACK, HALF], F32) for h in range(2)]
        asum = sb("asum", [P, 2, PACK, HALF], F32)
        z2_rows = sb("z2_rows", [P, PACK, H], BF16, tag="wa_g1")
        b_sb = [sb(f"b{t}", [P, H], F32, tag=["wa_raw0", "wa_g0", "", ""][t]) for t in range(PACK)]
        a_sb = [sb(f"a{t}", [P, H], F32) for t in range(PACK)]
        bgot = [sb(f"bgot{t}", [P, H], F32) for t in range(PACK)]
        agot = [sb(f"agot{t}", [P, H], F32) for t in range(PACK)]
        bsum = sb("bsum", [P, PACK, H], F32, tag="wa_raw1")
        old = []
        z2_g = sb("z2_g", [P, H, PACK], BF16)
        z2_c = sb("z2_c", [P, H], U32)
        z2_s = sb("z2_s", [P, H], U8)
        z_g = sb("z_g", [P, PACK, P, PACK], BF16)

        def b_copy(t):
            nc.scalar.copy(b_sb[t][:], b_ps[t][:])

        def b_gather(t):
            for h in range(2):
                gather("s", bgot[t][:, halves[h]], b_sb[t][:], n2_t[:, lhalves[h]])

        def b_add(t):
            nc.vector.tensor_tensor(bsum[:, t, :], b_ps[t][:], bgot[t][:], ALU.add)

        def z2_row(t):
            nc.gpsimd.tensor_scalar(z2_rows[:, t, :], b_sb[t][:], gi_t[:, t : t + 1], 0.0, ALU.mult, ALU.add)

        def a_copy(engine, t):
            if engine == "s":
                nc.scalar.activation(a_sb[t][:], a_ps[t][:], ACT.Copy, scale=gt_t[:, t : t + 1])
            else:
                nc.vector.tensor_scalar(a_sb[t][:], a_ps[t][:], gt_t[:, t : t + 1], None, ALU.mult)

        def a_gather(engine, t, h):
            gather(engine, agot[t][:, halves[h]], a_sb[t][:], n1_t[:, lhalves[h]])

        def a_add(t, h):
            nc.vector.scalar_tensor_tensor(
                asum[:, h, t, :], a_ps[t][:, halves[h]], gt_t[:, t : t + 1], agot[t][:, halves[h]], ALU.mult, ALU.add
            )

        def a_add_both(t):
            split = "p (h c) -> p h c"
            nc.vector.scalar_tensor_tensor(
                asum[:, :, t, :], a_ps[t][:].rearrange(split, h=2), gt_t[:, t : t + 1],
                agot[t][:].rearrange(split, h=2), ALU.mult, ALU.add,
            )

        def old_fetch(u):
            old.append(sb(f"old{u}", [P, H], F32, tag=["wa_raw1", "gate0", "gate1", "asum"][u]))
            nc.scalar.activation(old[u][:], page[u][:].indirect(n3_t[:]), ACT.Copy, scale=0.5)

        def a_gather_both(t):
            for h in range(2):
                a_gather("v", t, h)

        def z_half(h):
            nc.vector.tensor_tensor(
                z_g[:, :, h * 64 : (h + 1) * 64, :].rearrange("p u m t -> p m t u"),
                asum[:, h, :, :].rearrange("p t (m u) -> p m t u", u=PACK),
                gate[h][:].rearrange("p t (m u) -> p m t u", u=PACK),
                ALU.mult,
            )

        b_copy(0)
        b_copy(1)
        z2_row(0)
        z2_row(1)
        b_gather(0)
        a_copy("v", 0)
        a_gather_both(0)
        b_add(0)
        b_copy(2)
        z2_row(2)
        b_gather(1)
        a_copy("v", 2)
        a_add_both(0)
        b_add(1)
        b_copy(3)
        z2_row(3)
        nc.gpsimd.tensor_scalar(z2_g[:], z2_rows[:].rearrange("p t c -> p c t"), 1.0, 0.0, ALU.mult, ALU.add)
        a_copy("s", 1)
        b_gather(2)
        a_gather_both(1)
        b_add(2)
        b_gather(3)
        a_gather_both(2)
        b_add(3)
        a_copy("s", 3)
        a_add_both(1)
        a_add_both(2)
        for h in range(2):
            a_gather("s", 3, h)
            a_add(3, h)
            nc.scalar.activation(gate[h][:], bsum[:, :, halves[h]], ACT.Sigmoid)
            z_half(h)
            if h == 0:
                quantise(z2_c, z2_s, slice(0, H), z2_g[:])
        old_fetch(0)
        z_c = sb("z_c", [P, H], U32)
        z_s = sb("z_s", [P, H], U8)
        for u in range(PACK):
            cols = slice(u * P, (u + 1) * P)
            nc.vector.quantize_mx(
                out=z_c[:, cols].bitcast(FP8X4), scales=z_s[:, cols], in_=z_g[:, u, :, :].rearrange("p m t -> p (m t)")
            )
        cv_ps = [product("bcv", z_c, z_s, z2_c, z2_s, u) for u in range(PACK)]

        for u in range(1, PACK):
            old_fetch(u)
        parts = [slice(0, 640), slice(640, U)]
        widths = [c.stop - c.start for c in parts]
        y_rows = [[sb(f"y_rows{i}{e}", [P, 2, widths[i]], BF16) for e in range(2)] for i in range(2)]
        y_g = [sb(f"y_g{i}", [P, widths[i], PACK], BF16) for i in range(2)]
        y_c = sb("y_c", [P, U], U32)
        y_s = sb("y_s", [P, U], U8)
        words_out = out_1[0].rearrange("p n t -> p (n t)").bitcast(I32)

        def cast(copy, i, u):
            copy(y_rows[i][u // 2][:, u % 2, :], page[u][:, parts[i]])

        def weave(copy, i, e):
            copy(y_g[i][:, :, 2 * e : 2 * e + 2], y_rows[i][e][:].rearrange("p r c -> p c r"))

        for u in range(PACK):
            new = sb(f"new{u}", [P, H], F32)
            nc.vector.scalar_tensor_tensor(new[:], cv_ps[u][:], 0.0625, old[u][:], ALU.mult, ALU.max)
            nc.vector.tensor_copy(page[u][:].indirect(n3_t[:]), new[:])
            nc.sync.dma_start(out_0.rearrange("(p t) u -> p t u", t=PACK)[:, u, :], page[u][:])
            if u < PACK - 1:
                for i in range(2):
                    cast(nc.scalar.copy, i, u)
            if u == 1:
                for i in range(2):
                    weave(nc.scalar.copy, i, 0)
        cast(nc.scalar.copy, 1, PACK - 1)
        weave(nc.scalar.copy, 1, 1)
        cast(nc.vector.tensor_copy, 0, PACK - 1)
        weave(nc.vector.tensor_copy, 0, 1)
        for i, lo, hi in ((0, 0, 512), (0, 512, 640), (1, 640, U)):
            cols = slice(lo, hi)
            quantise(y_c, y_s, cols, y_g[i][:, lo - parts[i].start : hi - parts[i].start, :])
            nc.sync.dma_start(words_out[:, cols], y_c[:, cols].bitcast(I32))
        for q in range(4):
            nc.scalar.dma_start(out_2[0, 4 * q : 4 * q + 4, :].bitcast(I32), y_s[32 * q : 32 * q + 4, :].bitcast(I32))
